import numpy as np
import ml_dtypes


def mxq(x, axis, fmt="e4m3"):
    dtype, down = {"e4m3": (ml_dtypes.float8_e4m3fn, 7), "e5m2": (ml_dtypes.float8_e5m2, 14)}[fmt]
    v = np.moveaxis(np.asarray(x, np.float32).astype(ml_dtypes.bfloat16).astype(np.float64), axis, -1)
    blocks = v.reshape(v.shape[:-1] + (-1, 32))
    amax = np.abs(blocks).max(-1, keepdims=True)
    byte = np.maximum(np.where(amax > 0, np.frexp(amax)[1] - 1 + 127, 0) - down, 1)
    scale = np.exp2(byte - 127.0)
    codes = (blocks / scale).astype(np.float32).astype(dtype).astype(np.float64)
    return np.moveaxis((codes * scale).reshape(v.shape), -1, axis)


WIDE = False


def mx_kscale(k):
    if not WIDE:
        return np.ones(k)
    levels = np.array([10, -10, 5, -5, 0])
    if k % 512:
        return np.exp2(np.random.permutation(np.resize(levels, k // 32))).repeat(32)
    a = np.empty((k // 512, 16))
    for p in range(k // 512):
        a[p, :8] = np.random.permutation(np.resize(levels, 8))
        for g in range(8):
            far = levels[np.abs(levels - a[p, g]) >= 10]
            a[p, g + 8] = far[np.random.randint(len(far))]
    return np.exp2(a.ravel()).repeat(32)


def f64(x):
    return np.asarray(x).astype(np.float64)


def striped(idx):
    return np.tile(np.asarray(idx).reshape(-1, 16).T, (8, 1)).astype(np.uint16)


def unstriped(offs):
    return offs[:16].T.reshape(-1).astype(np.int64)


def sigmoid(v):
    return 1.0 / (1.0 + np.exp(-v))


D, T, I, Q, E = 512, 1024, 512, 128, 512


def setup_inputs():
    n = np.random.standard_normal
    idx = np.random.permutation(T)[:I]
    fd = mx_kscale(D)
    fi = mx_kscale(I)
    ti = np.ones(T)
    ti[idx] = fi
    return {
        "query": (n((D, Q)) * 0.4 / np.sqrt(D) * fd[:, None]).astype(np.float32),
        "keys": (n((D, T)) / fd[:, None]).astype(np.float32),
        "kgate": (n((D, T))).astype(np.float32),
        "size": (np.random.uniform(0.5, 2.0, (1, I)) * fi).astype(np.float32),
        "vals": (n((E, T)) / ti).astype(np.float32),
        "offs": striped(idx),
    }


def reference(query, keys, kgate, size, vals, offs):
    idx = unstriped(offs)
    km = f64(keys)[:, idx] * sigmoid(f64(kgate)[:, idx])
    queryq = mxq(f64(query), 0, "e4m3")
    kmq = mxq(km, 0, "e4m3")
    a = queryq.T @ kmq
    p = np.exp(a - np.max(a, axis=1, keepdims=True))
    w = p * f64(size) / np.sum(p, axis=1, keepdims=True)
    wt = w.T
    vt = f64(vals)[:, idx].T
    wtq = mxq(wt, 0, "e4m3")
    vtq = mxq(vt, 0, "e4m3")
    o = wtq.T @ vtq
    return o

@@ -1,0 +1,238 @@
+from contextlib import ExitStack
+
+import concourse.mybir as mybir
+from concourse.masks import make_identity
+
+D, T, I, Q, E = 512, 1024, 512, 128, 512
+FLOPS = 2 * Q * I * D + 2 * Q * I * E
+
+F32 = mybir.dt.float32
+BF16 = mybir.dt.bfloat16
+U32 = mybir.dt.uint32
+U16 = mybir.dt.uint16
+U8 = mybir.dt.uint8
+FP8X4 = mybir.dt.float8_e4m3fn_x4
+ACT = mybir.ActivationFunctionType
+ALU = mybir.AluOpType
+
+P = 128
+PACK = 4
+ORDER = ["g0","o","k0","s","g1","k1","v0","g2","k2","g3","q","k3","v1","v2","v3"]
+
+
+def tile_attend_gatedkeys_kernel(tc, query, keys, kgate, size, vals, offs, out):
+    nc = tc.nc
+    with ExitStack() as ctx:
+        keep = ctx.enter_context(tc.tile_pool(name="keep", bufs=1))
+        psum = ctx.enter_context(tc.psum_pool(name="psum", bufs=1))
+        turn = ctx.enter_context(tc.psum_pool(name="turn", bufs=3))
+
+        offsets = keep.tile([P, I // 16], U16, name="offsets")
+        gate_pool = [keep.tile([P, T], F32, name="gate_pool%d" % t, tag="gate_pool%d" % t, align_bytes=64) for t in range(PACK)]
+        key_pool = [keep.tile([P, T], F32, name="key_pool%d" % t) for t in range(PACK)]
+        val_pool = [keep.tile([P, T], F32, name="val_pool%d" % b, tag="val%d" % b) for b in range(E // P)]
+        query_raw = keep.tile([P, PACK, Q], F32, name="query_raw")
+        size_cols = keep.tile([P, PACK], F32, name="size_cols")
+        gate_planes = kgate.rearrange("(p t) n -> t p n", t=PACK)
+        key_planes = keys.rearrange("(p t) n -> t p n", t=PACK)
+        for item in ORDER:
+            if item == "o":
+                nc.sync.dma_start(offsets[:], offs)
+            elif item == "q":
+                nc.sync.dma_start(query_raw[:], query.rearrange("(p t) q -> p t q", t=PACK))
+            elif item == "s":
+                nc.sync.dma_start(size_cols[:], size.rearrange("o (s t) -> s (o t)", t=PACK))
+            elif item[0] == "g":
+                nc.sync.dma_start(gate_pool[int(item[1])][:], gate_planes[int(item[1])])
+            elif item[0] == "k":
+                nc.sync.dma_start(key_pool[int(item[1])][:], key_planes[int(item[1])])
+            else:
+                b = int(item[1])
+                nc.sync.dma_start(val_pool[b][:], vals[b * P : (b + 1) * P, :])
+
+        warm_in = keep.tile([P, 1], F32, name="warm_in")
+        nc.vector.memset(warm_in[:], 0.0)
+        warm_sig = keep.tile([P, 1], F32, name="warm_sig")
+        nc.scalar.activation(warm_sig[:], warm_in[:], ACT.Sigmoid)
+
+        ident = keep.tile([P, P], F32, name="ident")
+        make_identity(nc, ident[:])
+        size_rows = psum.tile([P, PACK, P], F32, name="size_rows")
+        for t in range(PACK):
+            nc.tensor.transpose(size_rows[:, t, :], size_cols[:, t : t + 1].to_broadcast([P, P]), ident[:])
+
+        km_grouped = keep.tile([P, I, PACK], BF16, name="km_grouped", align_bytes=64)
+        km_planes = keep.tile([P, PACK, I], F32, name="km_planes", tag="km1")
+        km = [km_planes[:, 0:2, :], km_planes[:, 2:4, :]]
+        gates = [keep.tile([P, I], F32, name="gate%d" % t) for t in range(PACK)]
+        km_codes = keep.tile([P, I], U32, name="km_codes", align_bytes=64)
+        km_scales = keep.tile([P, I], U8, name="km_scales", align_bytes=64)
+        q_grouped = keep.tile([P, Q, PACK], BF16, name="q_grouped", align_bytes=64)
+        q_codes = keep.tile([P, Q], U32, name="q_codes", align_bytes=64)
+        q_scales = keep.tile([P, Q], U8, name="q_scales", align_bytes=64)
+        scores = psum.tile([Q, I], F32, name="scores")
+        p_dealt = keep.tile([Q, 2, P, 2], F32, name="p_dealt", tag="p_dealt", align_bytes=64)
+        row_sum = keep.tile([Q, 1], F32, name="row_sum")
+        w_turned = psum.tile([P, 2, Q], F32, name="w_turned")
+        w_grouped = keep.tile([P, Q, PACK], BF16, name="w_grouped", align_bytes=64)
+        w_codes = keep.tile([P, Q], U32, name="w_codes", align_bytes=64)
+        w_scales = keep.tile([P, Q], U8, name="w_scales", align_bytes=64)
+        v_codes = {}
+        v_scales = [keep.tile([P, 2 * P], U8, name="v_scales%d" % h, align_bytes=64) for h in range(2)]
+        v_grouped = {}
+        made = {}
+
+        def sig(t):
+            nc.scalar.activation(gates[t][:], gate_pool[t][:].indirect(offsets[:]), ACT.Sigmoid)
+
+        def warmexp():
+            warm_exp = keep.tile([P, 1], F32, name="warm_exp")
+            nc.scalar.activation(warm_exp[:], gates[PACK - 1][:, 0:1], ACT.Exp)
+
+        def mul(t):
+            nc.vector.tensor_tensor(km[t // 2][:, t % 2, :], key_pool[t][:].indirect(offsets[:]), gates[t][:], ALU.mult)
+
+        def weave(pair):
+            nc.vector.tensor_copy(km_grouped[:, :, 2 * pair : 2 * pair + 2], km[pair][:].rearrange("p e i -> p i e"))
+
+        def weaveall():
+            nc.vector.tensor_copy(km_grouped[:].rearrange("p (c i) t -> p c t i", i=4),
+                                  km_planes[:].rearrange("p t (c i) -> p c t i", i=4))
+
+        def qcopy(engine):
+            if engine == "V":
+                nc.vector.tensor_copy(q_grouped[:], query_raw[:].rearrange("p t q -> p q t"))
+            else:
+                nc.scalar.copy(q_grouped[:], query_raw[:].rearrange("p t q -> p q t"))
+
+        def qquant():
+            nc.vector.quantize_mx(q_codes[:].bitcast(FP8X4), q_scales[:], q_grouped[:].rearrange("p q t -> p (q t)"))
+
+        def kquant():
+            nc.vector.quantize_mx(km_codes[:].bitcast(FP8X4), km_scales[:], km_grouped[:].rearrange("p i t -> p (i t)"))
+
+        def score():
+            nc.tensor.matmul_mx(scores[:], lhsT=q_codes[:].bitcast(FP8X4), lhsT_scale=q_scales[:],
+                                rhs=km_codes[:].bitcast(FP8X4), rhs_scale=km_scales[:], start=True, stop=True)
+
+        def pick(b, engine):
+            if b == 3:
+                picked = made["shared"][:, 16 : 16 + I]
+            else:
+                picked = keep.tile([P, I], BF16, name="picked%d" % b, tag={"2":"km1"}.get(str(b), "picked%d" % b))[:]
+            made["picked%d" % b] = picked
+            if engine == "S":
+                val_bf = keep.tile([P, T], BF16, name="val_bf%d" % b)
+                nc.scalar.activation(val_bf[:], val_pool[b][:], ACT.Copy)
+                nc.scalar.activation(picked, val_bf[:].indirect(offsets[:]), ACT.Copy)
+            else:
+                nc.vector.tensor_copy(picked, val_pool[b][:].indirect(offsets[:]))
+
+        def vturn(b):
+            words = made["picked%d" % b].bitcast(F32)
+            v_turned = turn.tile([P, 2, P], F32, name="v_turned")
+            made["turned%d" % b] = v_turned
+            for u in range(2):
+                nc.tensor.transpose(v_turned[:, u, :], words[:, u : I // 2 : 2], ident[:])
+
+        def vcopy(b):
+            if b % 2 == 0:
+                v_grouped[b // 2] = keep.tile([P, 2, P, PACK], BF16, name="v_grouped%d" % (b // 2), tag=["gate_pool3","vg1"][b // 2], align_bytes=64)
+            nc.scalar.copy(v_grouped[b // 2][:, b % 2, :, :].rearrange("s e t -> s (e t)").bitcast(F32).rearrange("s (e u) -> s e u", u=2),
+                           made["turned%d" % b][:].rearrange("s u e -> s e u"))
+
+        def vquant(b):
+            cols = slice((b % 2) * P, (b % 2 + 1) * P)
+            nc.vector.quantize_mx(v_codes[b // 2][:, cols].bitcast(FP8X4), v_scales[b // 2][:, cols],
+                                  v_grouped[b // 2][:, b % 2, :, :].rearrange("s e t -> s (e t)"))
+
+        def vquantpair(h, tag="own"):
+            v_codes[h] = keep.tile([P, 2 * P], U32, name="v_codes%d" % h, tag=tag, align_bytes=64)
+            nc.vector.quantize_mx(v_codes[h][:].bitcast(FP8X4), v_scales[h][:],
+                                  v_grouped[h][:].rearrange("s j e t -> s (j e t)"))
+
+        def rowmax(tag="neg_max"):
+            shared = keep.tile([P, 16 + I], BF16, name="shared", tag=tag)
+            made["shared"] = shared
+            neg_max = shared[:, 0:2].bitcast(F32)
+            made["neg_max"] = neg_max
+            nc.vector.tensor_reduce(neg_max, scores[:], mybir.AxisListType.X, ALU.max, negate=True)
+
+        def expo():
+            nc.scalar.activation(p_dealt[:], scores[:].rearrange("q (s u e) -> q u s e", u=2, e=2), ACT.Exp,
+                                 bias=made["neg_max"], accum_out=row_sum[:])
+
+        def recip(tag="inv_sum"):
+            inv_sum = keep.tile([Q, 1], F32, name="inv_sum", tag=tag)
+            made["inv_sum"] = inv_sum
+            nc.vector.reciprocal(inv_sum[:], row_sum[:])
+
+        def weigh(u):
+            w_half = keep.tile([Q, P, 2], BF16, name="w_half%d" % u)
+            nc.vector.scalar_tensor_tensor(w_half[:], p_dealt[:, u, :, :], made["inv_sum"][:],
+                                           size_rows[:, 2 * u : 2 * u + 2, :].rearrange("q e s -> q s e"),
+                                           ALU.mult, ALU.mult)
+            nc.tensor.transpose(w_turned[:, u, :], w_half[:].rearrange("q s e -> q (s e)").bitcast(F32), ident[:])
+
+        def wcopy():
+            nc.scalar.copy(w_grouped[:].rearrange("s q t -> s (q t)").bitcast(F32).rearrange("s (q u) -> s q u", u=2),
+                           w_turned[:].rearrange("s u q -> s q u"))
+
+        def wquant():
+            nc.vector.quantize_mx(w_codes[:].bitcast(FP8X4), w_scales[:], w_grouped[:].rearrange("s q t -> s (q t)"))
+
+        def outp(half):
+            acc = psum.tile([Q, 2 * P], F32, name="acc%d" % half)
+            nc.tensor.matmul_mx(acc[:], lhsT=w_codes[:].bitcast(FP8X4), lhsT_scale=w_scales[:],
+                                rhs=v_codes[half][:].bitcast(FP8X4), rhs_scale=v_scales[half][:], start=True, stop=True)
+            result = keep.tile([Q, 2 * P], F32, name="result%d" % half)
+            if half == 0:
+                nc.scalar.copy(result[:], acc[:])
+                nc.scalar.dma_start(out[:, 0 : 2 * P], result[:])
+            else:
+                nc.vector.tensor_copy(result[:], acc[:])
+                nc.sync.dma_start(out[:, 2 * P : 4 * P], result[:])
+
+        def clock(which):
+            tick = keep.tile([P, 1], F32, name="tick_" + which)
+            source = {"max": lambda: made["neg_max"], "w": lambda: w_grouped[:, 0, 0:1], "km": lambda: km[1][:, 1, 0:1],
+                      "kt": lambda: key_pool[3][:, 0:1], "vz": lambda: val_pool[0][:, 0:1], "gt": lambda: gates[3][:, 0:1], "kg": lambda: km_grouped[:, 0, 3:4], "inv": lambda: made["inv_sum"][:], "p": lambda: p_dealt[:, 0, 0, 0:1]}[which]()
+            nc.gpsimd.tensor_copy(tick[:], source)
+
+        sig(0)
+        mul(0)
+        sig(1)
+        mul(1)
+        pick(0, "V")
+        vturn(0)
+        sig(2)
+        mul(2)
+        sig(3)
+        vcopy(0)
+        warmexp()
+        qcopy("V")
+        qquant()
+        mul(3)
+        weaveall()
+        kquant()
+        score()
+        pick(1, "S")
+        vturn(1)
+        vcopy(1)
+        pick(2, "V")
+        vturn(2)
+        rowmax("val2")
+        pick(3, "V")
+        expo()
+        vcopy(2)
+        vturn(3)
+        recip("val3")
+        weigh(0)
+        weigh(1)
+        vcopy(3)
+        wcopy()
+        vquantpair(0, "p_dealt")
+        vquantpair(1)
+        wquant()
+        outp(0)
+        outp(1)

@@ -17,7 +17,8 @@ ALU = mybir.AluOpType
 
 P = 128
 PACK = 4
-ORDER = ["g0","o","k0","s","g1","k1","v0","g2","k2","g3","q","k3","v1","v2","v3"]
+H = I // 2
+ORDER = ["g0","o","k0","g1","g2","k1","g3","k2","k3","q","s","v0","v1","v2","v3"]
 
 
 def tile_attend_gatedkeys_kernel(tc, query, keys, kgate, size, vals, offs, out):
@@ -25,14 +26,16 @@ def tile_attend_gatedkeys_kernel(tc, query, keys, kgate, size, vals, offs, out):
     with ExitStack() as ctx:
         keep = ctx.enter_context(tc.tile_pool(name="keep", bufs=1))
         psum = ctx.enter_context(tc.psum_pool(name="psum", bufs=1))
-        turn = ctx.enter_context(tc.psum_pool(name="turn", bufs=3))
+
+        def sb(shape, dtype, name, tag=None):
+            return keep.tile(shape, dtype, name=name, tag=tag or name, align_bytes=64)
 
         offsets = keep.tile([P, I // 16], U16, name="offsets")
-        gate_pool = [keep.tile([P, T], F32, name="gate_pool%d" % t, tag="gate_pool%d" % t, align_bytes=64) for t in range(PACK)]
-        key_pool = [keep.tile([P, T], F32, name="key_pool%d" % t) for t in range(PACK)]
-        val_pool = [keep.tile([P, T], F32, name="val_pool%d" % b, tag="val%d" % b) for b in range(E // P)]
-        query_raw = keep.tile([P, PACK, Q], F32, name="query_raw")
-        size_cols = keep.tile([P, PACK], F32, name="size_cols")
+        gate_pool = [sb([P, T], F32, "gate_pool%d" % t) for t in range(PACK)]
+        key_pool = [sb([P, T], F32, "key_pool%d" % t) for t in range(PACK)]
+        val_pool = [sb([P, T], F32, "val_pool%d" % b) for b in range(E // P)]
+        query_raw = sb([P, PACK, Q], F32, "query_raw")
+        size_cols = sb([P, PACK], F32, "size_cols")
         gate_planes = kgate.rearrange("(p t) n -> t p n", t=PACK)
         key_planes = keys.rearrange("(p t) n -> t p n", t=PACK)
         for item in ORDER:
@@ -50,189 +53,197 @@ def tile_attend_gatedkeys_kernel(tc, query, keys, kgate, size, vals, offs, out):
                 b = int(item[1])
                 nc.sync.dma_start(val_pool[b][:], vals[b * P : (b + 1) * P, :])
 
-        warm_in = keep.tile([P, 1], F32, name="warm_in")
+        warm_in = sb([P, 1], F32, "warm_in")
         nc.vector.memset(warm_in[:], 0.0)
-        warm_sig = keep.tile([P, 1], F32, name="warm_sig")
+        warm_sig = sb([P, 1], F32, "warm_sig")
         nc.scalar.activation(warm_sig[:], warm_in[:], ACT.Sigmoid)
 
-        ident = keep.tile([P, P], F32, name="ident")
+        ident = sb([P, P], F32, "ident")
         make_identity(nc, ident[:])
         size_rows = psum.tile([P, PACK, P], F32, name="size_rows")
         for t in range(PACK):
             nc.tensor.transpose(size_rows[:, t, :], size_cols[:, t : t + 1].to_broadcast([P, P]), ident[:])
 
-        km_grouped = keep.tile([P, I, PACK], BF16, name="km_grouped", align_bytes=64)
-        km_planes = keep.tile([P, PACK, I], F32, name="km_planes", tag="km1")
-        km = [km_planes[:, 0:2, :], km_planes[:, 2:4, :]]
-        gates = [keep.tile([P, I], F32, name="gate%d" % t) for t in range(PACK)]
-        km_codes = keep.tile([P, I], U32, name="km_codes", align_bytes=64)
-        km_scales = keep.tile([P, I], U8, name="km_scales", align_bytes=64)
-        q_grouped = keep.tile([P, Q, PACK], BF16, name="q_grouped", align_bytes=64)
-        q_codes = keep.tile([P, Q], U32, name="q_codes", align_bytes=64)
-        q_scales = keep.tile([P, Q], U8, name="q_scales", align_bytes=64)
+        km = [sb([P, PACK, H], F32, "km%d" % h) for h in range(2)]
+        km_grouped = [sb([P, H, PACK], BF16, "km_grouped%d" % h) for h in range(2)]
+        km_codes = [sb([P, H], U32, "km_codes%d" % h) for h in range(2)]
+        km_scales = [sb([P, H], U8, "km_scales%d" % h) for h in range(2)]
+        gates = [sb([P, I], F32, "gate%d" % t) for t in range(PACK)]
+        q_grouped = sb([P, Q, PACK], BF16, "q_grouped")
+        q_codes = sb([P, Q], U32, "q_codes")
+        q_scales = sb([P, Q], U8, "q_scales")
         scores = psum.tile([Q, I], F32, name="scores")
-        p_dealt = keep.tile([Q, 2, P, 2], F32, name="p_dealt", tag="p_dealt", align_bytes=64)
-        row_sum = keep.tile([Q, 1], F32, name="row_sum")
+        row_sum = sb([Q, 1], F32, "row_sum")
         w_turned = psum.tile([P, 2, Q], F32, name="w_turned")
-        w_grouped = keep.tile([P, Q, PACK], BF16, name="w_grouped", align_bytes=64)
-        w_codes = keep.tile([P, Q], U32, name="w_codes", align_bytes=64)
-        w_scales = keep.tile([P, Q], U8, name="w_scales", align_bytes=64)
-        v_codes = {}
-        v_scales = [keep.tile([P, 2 * P], U8, name="v_scales%d" % h, align_bytes=64) for h in range(2)]
-        v_grouped = {}
+        w_grouped = sb([P, Q, PACK], BF16, "w_grouped")
+        w_codes = sb([P, Q], U32, "w_codes")
+        w_scales = sb([P, Q], U8, "w_scales")
+        v_codes = [sb([P, 2 * P], U32, "v_codes%d" % h) for h in range(2)]
+        v_scales = [sb([P, 2 * P], U8, "v_scales%d" % h) for h in range(2)]
         made = {}
+        eng = {"V": nc.vector.tensor_copy, "S": nc.scalar.copy}
 
         def sig(t):
             nc.scalar.activation(gates[t][:], gate_pool[t][:].indirect(offsets[:]), ACT.Sigmoid)
 
         def warmexp():
-            warm_exp = keep.tile([P, 1], F32, name="warm_exp")
+            warm_exp = sb([P, 1], F32, "warm_exp")
             nc.scalar.activation(warm_exp[:], gates[PACK - 1][:, 0:1], ACT.Exp)
 
         def mul(t):
-            nc.vector.tensor_tensor(km[t // 2][:, t % 2, :], key_pool[t][:].indirect(offsets[:]), gates[t][:], ALU.mult)
+            for h in range(2):
+                nc.vector.tensor_tensor(km[h][:, t, :], key_pool[t][:].indirect(offsets[:, h * H // 16 : (h + 1) * H // 16]),
+                                        gates[t][:, h * H : (h + 1) * H], ALU.mult)
 
-        def weave(pair):
-            nc.vector.tensor_copy(km_grouped[:, :, 2 * pair : 2 * pair + 2], km[pair][:].rearrange("p e i -> p i e"))
+        def weave(h, engine="V"):
+            eng[engine](km_grouped[h][:].rearrange("p (c i) t -> p c t i", i=4), km[h][:].rearrange("p t (c i) -> p c t i", i=4))
 
-        def weaveall():
-            nc.vector.tensor_copy(km_grouped[:].rearrange("p (c i) t -> p c t i", i=4),
-                                  km_planes[:].rearrange("p t (c i) -> p c t i", i=4))
+        def weavepair(h, pair):
+            nc.vector.tensor_copy(km_grouped[h][:, :, 2 * pair : 2 * pair + 2], km[h][:, 2 * pair : 2 * pair + 2, :].rearrange("p e i -> p i e"))
 
         def qcopy(engine):
-            if engine == "V":
-                nc.vector.tensor_copy(q_grouped[:], query_raw[:].rearrange("p t q -> p q t"))
-            else:
-                nc.scalar.copy(q_grouped[:], query_raw[:].rearrange("p t q -> p q t"))
+            eng[engine](q_grouped[:].rearrange("p (c i) t -> p c t i", i=4), query_raw[:].rearrange("p t (c i) -> p c t i", i=4))
 
         def qquant():
             nc.vector.quantize_mx(q_codes[:].bitcast(FP8X4), q_scales[:], q_grouped[:].rearrange("p q t -> p (q t)"))
 
-        def kquant():
-            nc.vector.quantize_mx(km_codes[:].bitcast(FP8X4), km_scales[:], km_grouped[:].rearrange("p i t -> p (i t)"))
+        def kquant(h):
+            nc.vector.quantize_mx(km_codes[h][:].bitcast(FP8X4), km_scales[h][:], km_grouped[h][:].rearrange("p i t -> p (i t)"))
 
-        def score():
-            nc.tensor.matmul_mx(scores[:], lhsT=q_codes[:].bitcast(FP8X4), lhsT_scale=q_scales[:],
-                                rhs=km_codes[:].bitcast(FP8X4), rhs_scale=km_scales[:], start=True, stop=True)
+        def score(h):
+            nc.tensor.matmul_mx(scores[:, h * H : (h + 1) * H], lhsT=q_codes[:].bitcast(FP8X4), lhsT_scale=q_scales[:],
+                                rhs=km_codes[h][:].bitcast(FP8X4), rhs_scale=km_scales[h][:], start=True, stop=True)
 
-        def pick(b, engine):
-            if b == 3:
-                picked = made["shared"][:, 16 : 16 + I]
-            else:
-                picked = keep.tile([P, I], BF16, name="picked%d" % b, tag={"2":"km1"}.get(str(b), "picked%d" % b))[:]
-            made["picked%d" % b] = picked
+        def cast(b, engine="S", tag=None):
+            val_bf = sb([P, T], BF16, "val_bf%d" % b, tag)
+            made["val_bf", b] = val_bf
             if engine == "S":
-                val_bf = keep.tile([P, T], BF16, name="val_bf%d" % b)
                 nc.scalar.activation(val_bf[:], val_pool[b][:], ACT.Copy)
-                nc.scalar.activation(picked, val_bf[:].indirect(offsets[:]), ACT.Copy)
             else:
-                nc.vector.tensor_copy(picked, val_pool[b][:].indirect(offsets[:]))
+                nc.vector.tensor_copy(val_bf[:], val_pool[b][:])
 
-        def vturn(b):
-            words = made["picked%d" % b].bitcast(F32)
-            v_turned = turn.tile([P, 2, P], F32, name="v_turned")
-            made["turned%d" % b] = v_turned
+        def picks(b, tag=None):
+            picked = sb([P, I], BF16, "picked%d" % b, tag)
+            made["picked", b] = picked
+            nc.scalar.activation(picked[:], made["val_bf", b][:].indirect(offsets[:]), ACT.Copy)
+
+        def pickv(b, tag=None):
+            picked = sb([P, I], BF16, "picked%d" % b, tag)
+            made["picked", b] = picked
+            nc.vector.tensor_copy(picked[:], val_pool[b][:].indirect(offsets[:]))
+
+        def vturn(b, bank):
+            words = made["picked", b][:].bitcast(F32)
+            if ("bank", bank) not in made:
+                made["bank", bank] = psum.tile([P, 2, 2, P], F32, name="v_turned%d" % bank)
             for u in range(2):
-                nc.tensor.transpose(v_turned[:, u, :], words[:, u : I // 2 : 2], ident[:])
+                nc.tensor.transpose(made["bank", bank][:, b % 2, u, :], words[:, u : I // 2 : 2], ident[:])
 
-        def vcopy(b):
-            if b % 2 == 0:
-                v_grouped[b // 2] = keep.tile([P, 2, P, PACK], BF16, name="v_grouped%d" % (b // 2), tag=["gate_pool3","vg1"][b // 2], align_bytes=64)
-            nc.scalar.copy(v_grouped[b // 2][:, b % 2, :, :].rearrange("s e t -> s (e t)").bitcast(F32).rearrange("s (e u) -> s e u", u=2),
-                           made["turned%d" % b][:].rearrange("s u e -> s e u"))
+        def grouped(h, tag):
+            if ("grouped", h) not in made:
+                made["grouped", h] = sb([P, 2, P, PACK], BF16, "v_grouped%d" % h, tag)
+            return made["grouped", h][:].rearrange("s j e t -> s (j e t)").bitcast(F32).rearrange("s (j e u) -> s j e u", j=2, u=2)
+
+        def vcopy(b, bank, engine, tag=None):
+            eng[engine](grouped(b // 2, tag)[:, b % 2, :, :], made["bank", bank][:, b % 2, :, :].rearrange("s u e -> s e u"))
+
+        def vcopypair(h, bank, engine, tag=None):
+            eng[engine](grouped(h, tag), made["bank", bank][:].rearrange("s j u e -> s j e u"))
+
+        def vquantpair(h):
+            nc.vector.quantize_mx(v_codes[h][:].bitcast(FP8X4), v_scales[h][:],
+                                  made["grouped", h][:].rearrange("s j e t -> s (j e t)"))
 
         def vquant(b):
             cols = slice((b % 2) * P, (b % 2 + 1) * P)
             nc.vector.quantize_mx(v_codes[b // 2][:, cols].bitcast(FP8X4), v_scales[b // 2][:, cols],
-                                  v_grouped[b // 2][:, b % 2, :, :].rearrange("s e t -> s (e t)"))
+                                  made["grouped", b // 2][:, b % 2, :, :].rearrange("s e t -> s (e t)"))
 
-        def vquantpair(h, tag="own"):
-            v_codes[h] = keep.tile([P, 2 * P], U32, name="v_codes%d" % h, tag=tag, align_bytes=64)
-            nc.vector.quantize_mx(v_codes[h][:].bitcast(FP8X4), v_scales[h][:],
-                                  v_grouped[h][:].rearrange("s j e t -> s (j e t)"))
-
-        def rowmax(tag="neg_max"):
-            shared = keep.tile([P, 16 + I], BF16, name="shared", tag=tag)
-            made["shared"] = shared
-            neg_max = shared[:, 0:2].bitcast(F32)
+        def rowmax(tag=None):
+            neg_max = sb([Q, 1], F32, "neg_max", tag)
             made["neg_max"] = neg_max
-            nc.vector.tensor_reduce(neg_max, scores[:], mybir.AxisListType.X, ALU.max, negate=True)
+            nc.vector.tensor_reduce(neg_max[:], scores[:], mybir.AxisListType.X, ALU.max, negate=True)
 
-        def expo():
+        def expo(tag=None):
+            p_dealt = sb([Q, 2, P, 2], F32, "p_dealt", tag)
+            made["p"] = p_dealt
             nc.scalar.activation(p_dealt[:], scores[:].rearrange("q (s u e) -> q u s e", u=2, e=2), ACT.Exp,
-                                 bias=made["neg_max"], accum_out=row_sum[:])
+                                 bias=made["neg_max"][:], accum_out=row_sum[:])
 
-        def recip(tag="inv_sum"):
-            inv_sum = keep.tile([Q, 1], F32, name="inv_sum", tag=tag)
+        def recip(tag=None):
+            inv_sum = sb([Q, 1], F32, "inv_sum", tag)
             made["inv_sum"] = inv_sum
             nc.vector.reciprocal(inv_sum[:], row_sum[:])
 
         def weigh(u):
-            w_half = keep.tile([Q, P, 2], BF16, name="w_half%d" % u)
-            nc.vector.scalar_tensor_tensor(w_half[:], p_dealt[:, u, :, :], made["inv_sum"][:],
+            w_half = sb([Q, P, 2], BF16, "w_half%d" % u)
+            nc.vector.scalar_tensor_tensor(w_half[:], made["p"][:, u, :, :], made["inv_sum"][:],
                                            size_rows[:, 2 * u : 2 * u + 2, :].rearrange("q e s -> q s e"),
                                            ALU.mult, ALU.mult)
             nc.tensor.transpose(w_turned[:, u, :], w_half[:].rearrange("q s e -> q (s e)").bitcast(F32), ident[:])
 
-        def wcopy():
-            nc.scalar.copy(w_grouped[:].rearrange("s q t -> s (q t)").bitcast(F32).rearrange("s (q u) -> s q u", u=2),
-                           w_turned[:].rearrange("s u q -> s q u"))
+        def wcopy(engine="S"):
+            eng[engine](w_grouped[:].rearrange("s q t -> s (q t)").bitcast(F32).rearrange("s (q u) -> s q u", u=2),
+                        w_turned[:].rearrange("s u q -> s q u"))
 
         def wquant():
             nc.vector.quantize_mx(w_codes[:].bitcast(FP8X4), w_scales[:], w_grouped[:].rearrange("s q t -> s (q t)"))
 
-        def outp(half):
+        def outp(half, engine):
             acc = psum.tile([Q, 2 * P], F32, name="acc%d" % half)
             nc.tensor.matmul_mx(acc[:], lhsT=w_codes[:].bitcast(FP8X4), lhsT_scale=w_scales[:],
                                 rhs=v_codes[half][:].bitcast(FP8X4), rhs_scale=v_scales[half][:], start=True, stop=True)
-            result = keep.tile([Q, 2 * P], F32, name="result%d" % half)
-            if half == 0:
-                nc.scalar.copy(result[:], acc[:])
-                nc.scalar.dma_start(out[:, 0 : 2 * P], result[:])
-            else:
-                nc.vector.tensor_copy(result[:], acc[:])
-                nc.sync.dma_start(out[:, 2 * P : 4 * P], result[:])
+            result = sb([Q, 2 * P], F32, "result%d" % half)
+            eng[engine](result[:], acc[:])
+            queue = nc.scalar if engine == "S" else nc.sync
+            queue.dma_start(out[:, half * 2 * P : (half + 1) * 2 * P], result[:])
 
         def clock(which):
-            tick = keep.tile([P, 1], F32, name="tick_" + which)
-            source = {"max": lambda: made["neg_max"], "w": lambda: w_grouped[:, 0, 0:1], "km": lambda: km[1][:, 1, 0:1],
-                      "kt": lambda: key_pool[3][:, 0:1], "vz": lambda: val_pool[0][:, 0:1], "gt": lambda: gates[3][:, 0:1], "kg": lambda: km_grouped[:, 0, 3:4], "inv": lambda: made["inv_sum"][:], "p": lambda: p_dealt[:, 0, 0, 0:1]}[which]()
+            tick = sb([P, 1], F32, "tick_" + which)
+            source = {"max": lambda: made["neg_max"][:], "w": lambda: w_grouped[:, 0, 0:1], "kg": lambda: km_grouped[1][:, 0, 0:1],
+                      "inv": lambda: made["inv_sum"][:], "p": lambda: made["p"][:, 0, 0, 0:1]}[which]()
             nc.gpsimd.tensor_copy(tick[:], source)
 
         sig(0)
         mul(0)
         sig(1)
-        mul(1)
-        pick(0, "V")
-        vturn(0)
         sig(2)
-        mul(2)
+        mul(1)
+        weavepair(0, 0)
+        weavepair(1, 0)
         sig(3)
-        vcopy(0)
         warmexp()
-        qcopy("V")
-        qquant()
+        mul(2)
         mul(3)
-        weaveall()
-        kquant()
-        score()
-        pick(1, "S")
-        vturn(1)
-        vcopy(1)
-        pick(2, "V")
-        vturn(2)
-        rowmax("val2")
-        pick(3, "V")
-        expo()
-        vcopy(2)
-        vturn(3)
-        recip("val3")
+        qcopy("S")
+        weavepair(0, 1)
+        weavepair(1, 1)
+        kquant(0)
+        qquant()
+        kquant(1)
+        score(0)
+        score(1)
+        cast(0)
+        picks(0)
+        vturn(0, 0)
+        pickv(1, "km_grouped0")
+        vturn(1, 0)
+        rowmax("val_pool1")
+        cast(2)
+        pickv(3)
+        vturn(3, 1)
+        expo("val_pool2")
+        picks(2)
+        vturn(2, 2)
+        recip("val_pool3")
         weigh(0)
         weigh(1)
-        vcopy(3)
+        vcopy(3, 1, "S")
         wcopy()
-        vquantpair(0, "p_dealt")
+        vcopypair(0, 0, "V", "row_sum")
+        vcopy(2, 2, "V")
+        vquantpair(0)
         vquantpair(1)
         wquant()
-        outp(0)
-        outp(1)
+        outp(0, "S")
+        outp(1, "V")

@@ -18,7 +18,7 @@ ALU = mybir.AluOpType
 P = 128
 PACK = 4
 H = I // 2
-ORDER = ["g0","o","k0","g1","g2","k1","g3","k2","k3","q","s","v0","v1","v2","v3"]
+ORDER = ["g0","o","k0","g1","g2","k1","g3","k2","q","k3","s","v0","v1","v2","v3"]
 
 
 def tile_attend_gatedkeys_kernel(tc, query, keys, kgate, size, vals, offs, out):
@@ -214,12 +214,12 @@ def tile_attend_gatedkeys_kernel(tc, query, keys, kgate, size, vals, offs, out):
         sig(3)
         warmexp()
         mul(2)
-        mul(3)
         qcopy("S")
+        qquant()
+        mul(3)
         weavepair(0, 1)
         weavepair(1, 1)
         kquant(0)
-        qquant()
         kquant(1)
         score(0)
         score(1)
@@ -228,14 +228,14 @@ def tile_attend_gatedkeys_kernel(tc, query, keys, kgate, size, vals, offs, out):
         vturn(0, 0)
         pickv(1, "km_grouped0")
         vturn(1, 0)
-        rowmax("val_pool1")
+        rowmax("val_bf0")
         cast(2)
         pickv(3)
         vturn(3, 1)
-        expo("val_pool2")
+        expo()
         picks(2)
         vturn(2, 2)
-        recip("val_pool3")
+        recip()
         weigh(0)
         weigh(1)
         vcopy(3, 1, "S")

@@ -17,8 +17,9 @@ ALU = mybir.AluOpType
 
 P = 128
 PACK = 4
-H = I // 2
-ORDER = ["g0","o","k0","g1","g2","k1","g3","k2","q","k3","s","v0","v1","v2","v3"]
+HALF = I // 2
+LIST_ROWS = 16
+ALIGN = 256
 
 
 def tile_attend_gatedkeys_kernel(tc, query, keys, kgate, size, vals, offs, out):
@@ -27,223 +28,176 @@ def tile_attend_gatedkeys_kernel(tc, query, keys, kgate, size, vals, offs, out):
         keep = ctx.enter_context(tc.tile_pool(name="keep", bufs=1))
         psum = ctx.enter_context(tc.psum_pool(name="psum", bufs=1))
 
-        def sb(shape, dtype, name, tag=None):
-            return keep.tile(shape, dtype, name=name, tag=tag or name, align_bytes=64)
+        def sbuf(shape, dtype, name, in_place_of=None):
+            return keep.tile(shape, dtype, name=name, tag=in_place_of or name, align_bytes=ALIGN)
 
-        offsets = keep.tile([P, I // 16], U16, name="offsets")
-        gate_pool = [sb([P, T], F32, "gate_pool%d" % t) for t in range(PACK)]
-        key_pool = [sb([P, T], F32, "key_pool%d" % t) for t in range(PACK)]
-        val_pool = [sb([P, T], F32, "val_pool%d" % b) for b in range(E // P)]
-        query_raw = sb([P, PACK, Q], F32, "query_raw")
-        size_cols = sb([P, PACK], F32, "size_cols")
+        def bank(shape, name, in_place_of=None):
+            return psum.tile(shape, F32, name=name, tag=in_place_of or name)
+
+        def quantise(codes, scales, grouped):
+            nc.vector.quantize_mx(codes.bitcast(FP8X4), scales, grouped)
+
+        def product(acc, lhs_codes, lhs_scales, rhs_codes, rhs_scales):
+            nc.tensor.matmul_mx(acc, lhsT=lhs_codes.bitcast(FP8X4), lhsT_scale=lhs_scales,
+                                rhs=rhs_codes.bitcast(FP8X4), rhs_scale=rhs_scales, start=True, stop=True)
+
+        offsets = keep.tile([P, I // LIST_ROWS], U16, name="offsets")
+        gate_pool = [sbuf([P, T], F32, "gate_pool%d" % t) for t in range(PACK)]
+        key_pool = [sbuf([P, T], F32, "key_pool%d" % t) for t in range(PACK)]
+        val_pool = [sbuf([P, T], F32, "val_pool%d" % b) for b in range(E // P)]
+        query_raw = sbuf([P, PACK, Q], F32, "query_raw")
+        size_cols = sbuf([P, PACK], F32, "size_cols")
         gate_planes = kgate.rearrange("(p t) n -> t p n", t=PACK)
         key_planes = keys.rearrange("(p t) n -> t p n", t=PACK)
-        for item in ORDER:
-            if item == "o":
-                nc.sync.dma_start(offsets[:], offs)
-            elif item == "q":
-                nc.sync.dma_start(query_raw[:], query.rearrange("(p t) q -> p t q", t=PACK))
-            elif item == "s":
-                nc.sync.dma_start(size_cols[:], size.rearrange("o (s t) -> s (o t)", t=PACK))
-            elif item[0] == "g":
-                nc.sync.dma_start(gate_pool[int(item[1])][:], gate_planes[int(item[1])])
-            elif item[0] == "k":
-                nc.sync.dma_start(key_pool[int(item[1])][:], key_planes[int(item[1])])
-            else:
-                b = int(item[1])
-                nc.sync.dma_start(val_pool[b][:], vals[b * P : (b + 1) * P, :])
 
-        warm_in = sb([P, 1], F32, "warm_in")
-        nc.vector.memset(warm_in[:], 0.0)
-        warm_sig = sb([P, 1], F32, "warm_sig")
-        nc.scalar.activation(warm_sig[:], warm_in[:], ACT.Sigmoid)
+        nc.sync.dma_start(gate_pool[0][:], gate_planes[0])
+        nc.sync.dma_start(offsets[:], offs)
+        nc.sync.dma_start(key_pool[0][:], key_planes[0])
+        nc.sync.dma_start(gate_pool[1][:], gate_planes[1])
+        for t in range(1, PACK - 1):
+            nc.sync.dma_start(gate_pool[t + 1][:], gate_planes[t + 1])
+            nc.sync.dma_start(key_pool[t][:], key_planes[t])
+        nc.sync.dma_start(key_pool[PACK - 1][:], key_planes[PACK - 1])
+        nc.sync.dma_start(query_raw[:], query.rearrange("(p t) q -> p t q", t=PACK))
+        nc.sync.dma_start(size_cols[:], size.rearrange("o (s t) -> s (o t)", t=PACK))
+        for b in range(E // P):
+            nc.sync.dma_start(val_pool[b][:], vals[b * P : (b + 1) * P, :])
 
-        ident = sb([P, P], F32, "ident")
+        ident = sbuf([P, P], F32, "ident")
         make_identity(nc, ident[:])
-        size_rows = psum.tile([P, PACK, P], F32, name="size_rows")
+        size_rows = bank([P, PACK, P], "size_rows")
         for t in range(PACK):
             nc.tensor.transpose(size_rows[:, t, :], size_cols[:, t : t + 1].to_broadcast([P, P]), ident[:])
 
-        km = [sb([P, PACK, H], F32, "km%d" % h) for h in range(2)]
-        km_grouped = [sb([P, H, PACK], BF16, "km_grouped%d" % h) for h in range(2)]
-        km_codes = [sb([P, H], U32, "km_codes%d" % h) for h in range(2)]
-        km_scales = [sb([P, H], U8, "km_scales%d" % h) for h in range(2)]
-        gates = [sb([P, I], F32, "gate%d" % t) for t in range(PACK)]
-        q_grouped = sb([P, Q, PACK], BF16, "q_grouped")
-        q_codes = sb([P, Q], U32, "q_codes")
-        q_scales = sb([P, Q], U8, "q_scales")
-        scores = psum.tile([Q, I], F32, name="scores")
-        row_sum = sb([Q, 1], F32, "row_sum")
-        w_turned = psum.tile([P, 2, Q], F32, name="w_turned")
-        w_grouped = sb([P, Q, PACK], BF16, "w_grouped")
-        w_codes = sb([P, Q], U32, "w_codes")
-        w_scales = sb([P, Q], U8, "w_scales")
-        v_codes = [sb([P, 2 * P], U32, "v_codes%d" % h) for h in range(2)]
-        v_scales = [sb([P, 2 * P], U8, "v_scales%d" % h) for h in range(2)]
-        made = {}
-        eng = {"V": nc.vector.tensor_copy, "S": nc.scalar.copy}
+        km = [sbuf([P, PACK, HALF], F32, "km%d" % h) for h in range(2)]
+        km_grouped = [sbuf([P, HALF, PACK], BF16, "km_grouped%d" % h) for h in range(2)]
+        km_codes = [sbuf([P, HALF], U32, "km_codes%d" % h) for h in range(2)]
+        km_scales = [sbuf([P, HALF], U8, "km_scales%d" % h) for h in range(2)]
+        gates = [sbuf([P, I], F32, "gate%d" % t) for t in range(PACK)]
 
-        def sig(t):
+        def gather_gates(t):
             nc.scalar.activation(gates[t][:], gate_pool[t][:].indirect(offsets[:]), ACT.Sigmoid)
 
-        def warmexp():
-            warm_exp = sb([P, 1], F32, "warm_exp")
-            nc.scalar.activation(warm_exp[:], gates[PACK - 1][:, 0:1], ACT.Exp)
-
-        def mul(t):
+        def gather_keys(t):
             for h in range(2):
-                nc.vector.tensor_tensor(km[h][:, t, :], key_pool[t][:].indirect(offsets[:, h * H // 16 : (h + 1) * H // 16]),
-                                        gates[t][:, h * H : (h + 1) * H], ALU.mult)
+                entries = offsets[:, h * HALF // LIST_ROWS : (h + 1) * HALF // LIST_ROWS]
+                nc.vector.tensor_tensor(km[h][:, t, :], key_pool[t][:].indirect(entries),
+                                        gates[t][:, h * HALF : (h + 1) * HALF], ALU.mult)
 
-        def weave(h, engine="V"):
-            eng[engine](km_grouped[h][:].rearrange("p (c i) t -> p c t i", i=4), km[h][:].rearrange("p t (c i) -> p c t i", i=4))
+        def group_planes(first):
+            for h in range(2):
+                nc.vector.tensor_copy(km_grouped[h][:, :, first : first + 2],
+                                      km[h][:, first : first + 2, :].rearrange("p t i -> p i t"))
 
-        def weavepair(h, pair):
-            nc.vector.tensor_copy(km_grouped[h][:, :, 2 * pair : 2 * pair + 2], km[h][:, 2 * pair : 2 * pair + 2, :].rearrange("p e i -> p i e"))
+        gather_gates(0)
+        gather_keys(0)
+        gather_gates(1)
+        gather_gates(2)
+        gather_keys(1)
+        group_planes(0)
+        gather_gates(3)
+        warm_exp = sbuf([P, 1], F32, "warm_exp")
+        nc.scalar.activation(warm_exp[:], gates[PACK - 1][:, 0:1], ACT.Exp)
+        gather_keys(2)
+        gather_keys(3)
 
-        def qcopy(engine):
-            eng[engine](q_grouped[:].rearrange("p (c i) t -> p c t i", i=4), query_raw[:].rearrange("p t (c i) -> p c t i", i=4))
+        q_grouped = sbuf([P, Q, PACK], BF16, "q_grouped")
+        q_codes = sbuf([P, Q], U32, "q_codes")
+        q_scales = sbuf([P, Q], U8, "q_scales")
+        nc.scalar.copy(q_grouped[:].rearrange("p (c j) t -> p c t j", j=4),
+                       query_raw[:].rearrange("p t (c j) -> p c t j", j=4))
+        group_planes(2)
+        quantise(km_codes[0][:], km_scales[0][:], km_grouped[0][:].rearrange("p i t -> p (i t)"))
+        quantise(q_codes[:], q_scales[:], q_grouped[:].rearrange("p q t -> p (q t)"))
+        quantise(km_codes[1][:], km_scales[1][:], km_grouped[1][:].rearrange("p i t -> p (i t)"))
 
-        def qquant():
-            nc.vector.quantize_mx(q_codes[:].bitcast(FP8X4), q_scales[:], q_grouped[:].rearrange("p q t -> p (q t)"))
+        scores = bank([Q, I], "scores")
+        for h in range(2):
+            product(scores[:, h * HALF : (h + 1) * HALF], q_codes[:], q_scales[:], km_codes[h][:], km_scales[h][:])
 
-        def kquant(h):
-            nc.vector.quantize_mx(km_codes[h][:].bitcast(FP8X4), km_scales[h][:], km_grouped[h][:].rearrange("p i t -> p (i t)"))
+        def cast_values(b):
+            val_bf = sbuf([P, T], BF16, "val_bf%d" % b)
+            nc.scalar.activation(val_bf[:], val_pool[b][:], ACT.Copy)
+            return val_bf
 
-        def score(h):
-            nc.tensor.matmul_mx(scores[:, h * H : (h + 1) * H], lhsT=q_codes[:].bitcast(FP8X4), lhsT_scale=q_scales[:],
-                                rhs=km_codes[h][:].bitcast(FP8X4), rhs_scale=km_scales[h][:], start=True, stop=True)
+        def gather_values_scalar(b, val_bf):
+            picked = sbuf([P, I], BF16, "picked%d" % b)
+            nc.scalar.activation(picked[:], val_bf[:].indirect(offsets[:]), ACT.Copy)
+            return picked
 
-        def cast(b, engine="S", tag=None):
-            val_bf = sb([P, T], BF16, "val_bf%d" % b, tag)
-            made["val_bf", b] = val_bf
-            if engine == "S":
-                nc.scalar.activation(val_bf[:], val_pool[b][:], ACT.Copy)
-            else:
-                nc.vector.tensor_copy(val_bf[:], val_pool[b][:])
-
-        def picks(b, tag=None):
-            picked = sb([P, I], BF16, "picked%d" % b, tag)
-            made["picked", b] = picked
-            nc.scalar.activation(picked[:], made["val_bf", b][:].indirect(offsets[:]), ACT.Copy)
-
-        def pickv(b, tag=None):
-            picked = sb([P, I], BF16, "picked%d" % b, tag)
-            made["picked", b] = picked
+        def gather_values_vector(b, in_place_of=None):
+            picked = sbuf([P, I], BF16, "picked%d" % b, in_place_of)
             nc.vector.tensor_copy(picked[:], val_pool[b][:].indirect(offsets[:]))
+            return picked
 
-        def vturn(b, bank):
-            words = made["picked", b][:].bitcast(F32)
-            if ("bank", bank) not in made:
-                made["bank", bank] = psum.tile([P, 2, 2, P], F32, name="v_turned%d" % bank)
+        def turn_values(turned, picked):
+            pairs = picked[:].bitcast(F32)
             for u in range(2):
-                nc.tensor.transpose(made["bank", bank][:, b % 2, u, :], words[:, u : I // 2 : 2], ident[:])
+                nc.tensor.transpose(turned[:, u, :], pairs[:, u : I // 2 : 2], ident[:])
 
-        def grouped(h, tag):
-            if ("grouped", h) not in made:
-                made["grouped", h] = sb([P, 2, P, PACK], BF16, "v_grouped%d" % h, tag)
-            return made["grouped", h][:].rearrange("s j e t -> s (j e t)").bitcast(F32).rearrange("s (j e u) -> s j e u", j=2, u=2)
+        turned_low = bank([P, 2, 2, P], "turned_low")
+        turn_values(turned_low[:, 0, :, :], gather_values_scalar(0, cast_values(0)))
+        turn_values(turned_low[:, 1, :, :], gather_values_vector(1, "km_grouped0"))
 
-        def vcopy(b, bank, engine, tag=None):
-            eng[engine](grouped(b // 2, tag)[:, b % 2, :, :], made["bank", bank][:, b % 2, :, :].rearrange("s u e -> s e u"))
+        neg_max = sbuf([Q, 1], F32, "neg_max", "val_bf0")
+        nc.vector.tensor_reduce(neg_max[:], scores[:], mybir.AxisListType.X, ALU.max, negate=True)
 
-        def vcopypair(h, bank, engine, tag=None):
-            eng[engine](grouped(h, tag), made["bank", bank][:].rearrange("s j u e -> s j e u"))
+        val_bf2 = cast_values(2)
+        turned3 = bank([P, 2, P], "turned3")
+        turn_values(turned3[:], gather_values_vector(3))
 
-        def vquantpair(h):
-            nc.vector.quantize_mx(v_codes[h][:].bitcast(FP8X4), v_scales[h][:],
-                                  made["grouped", h][:].rearrange("s j e t -> s (j e t)"))
+        p_dealt = sbuf([Q, 2, P, 2], F32, "p_dealt")
+        row_sum = sbuf([Q, 1], F32, "row_sum")
+        nc.scalar.activation(p_dealt[:], scores[:].rearrange("q (s u j) -> q u s j", u=2, j=2), ACT.Exp,
+                             bias=neg_max[:], accum_out=row_sum[:])
+        picked2 = gather_values_scalar(2, val_bf2)
 
-        def vquant(b):
-            cols = slice((b % 2) * P, (b % 2 + 1) * P)
-            nc.vector.quantize_mx(v_codes[b // 2][:, cols].bitcast(FP8X4), v_scales[b // 2][:, cols],
-                                  made["grouped", b // 2][:, b % 2, :, :].rearrange("s e t -> s (e t)"))
-
-        def rowmax(tag=None):
-            neg_max = sb([Q, 1], F32, "neg_max", tag)
-            made["neg_max"] = neg_max
-            nc.vector.tensor_reduce(neg_max[:], scores[:], mybir.AxisListType.X, ALU.max, negate=True)
-
-        def expo(tag=None):
-            p_dealt = sb([Q, 2, P, 2], F32, "p_dealt", tag)
-            made["p"] = p_dealt
-            nc.scalar.activation(p_dealt[:], scores[:].rearrange("q (s u e) -> q u s e", u=2, e=2), ACT.Exp,
-                                 bias=made["neg_max"][:], accum_out=row_sum[:])
-
-        def recip(tag=None):
-            inv_sum = sb([Q, 1], F32, "inv_sum", tag)
-            made["inv_sum"] = inv_sum
-            nc.vector.reciprocal(inv_sum[:], row_sum[:])
-
-        def weigh(u):
-            w_half = sb([Q, P, 2], BF16, "w_half%d" % u)
-            nc.vector.scalar_tensor_tensor(w_half[:], made["p"][:, u, :, :], made["inv_sum"][:],
-                                           size_rows[:, 2 * u : 2 * u + 2, :].rearrange("q e s -> q s e"),
+        inv_sum = sbuf([Q, 1], F32, "inv_sum")
+        nc.vector.reciprocal(inv_sum[:], row_sum[:])
+        w_turned = bank([P, 2, Q], "w_turned")
+        for u in range(2):
+            w_pairs = sbuf([Q, P, 2], BF16, "w_pairs%d" % u)
+            nc.vector.scalar_tensor_tensor(w_pairs[:], p_dealt[:, u, :, :], inv_sum[:],
+                                           size_rows[:, 2 * u : 2 * u + 2, :].rearrange("q j s -> q s j"),
                                            ALU.mult, ALU.mult)
-            nc.tensor.transpose(w_turned[:, u, :], w_half[:].rearrange("q s e -> q (s e)").bitcast(F32), ident[:])
+            nc.tensor.transpose(w_turned[:, u, :], w_pairs[:].rearrange("q s j -> q (s j)").bitcast(F32), ident[:])
 
-        def wcopy(engine="S"):
-            eng[engine](w_grouped[:].rearrange("s q t -> s (q t)").bitcast(F32).rearrange("s (q u) -> s q u", u=2),
-                        w_turned[:].rearrange("s u q -> s q u"))
+        turned2 = bank([P, 2, P], "turned2", "size_rows")
+        turn_values(turned2[:], picked2)
 
-        def wquant():
-            nc.vector.quantize_mx(w_codes[:].bitcast(FP8X4), w_scales[:], w_grouped[:].rearrange("s q t -> s (q t)"))
+        def as_pairs(grouped):
+            blocks = grouped.shape[1]
+            words = grouped[:].rearrange("s b c t -> s (b c t)").bitcast(F32)
+            return words.rearrange("s (b c u) -> s b c u", b=blocks, u=2)
 
-        def outp(half, engine):
-            acc = psum.tile([Q, 2 * P], F32, name="acc%d" % half)
-            nc.tensor.matmul_mx(acc[:], lhsT=w_codes[:].bitcast(FP8X4), lhsT_scale=w_scales[:],
-                                rhs=v_codes[half][:].bitcast(FP8X4), rhs_scale=v_scales[half][:], start=True, stop=True)
-            result = sb([Q, 2 * P], F32, "result%d" % half)
-            eng[engine](result[:], acc[:])
-            queue = nc.scalar if engine == "S" else nc.sync
-            queue.dma_start(out[:, half * 2 * P : (half + 1) * 2 * P], result[:])
+        v_high = sbuf([P, 2, P, PACK], BF16, "v_high")
+        w_grouped = sbuf([P, 1, Q, PACK], BF16, "w_grouped")
+        nc.scalar.copy(as_pairs(v_high)[:, 1, :, :], turned3[:].rearrange("s u e -> s e u"))
+        nc.scalar.copy(as_pairs(w_grouped)[:, 0, :, :], w_turned[:].rearrange("s u q -> s q u"))
+        nc.scalar.copy(as_pairs(v_high)[:, 0, :, :], turned2[:].rearrange("s u e -> s e u"))
+        v_low = sbuf([P, 2, P, PACK], BF16, "v_low", "row_sum")
+        nc.vector.tensor_copy(as_pairs(v_low), turned_low[:].rearrange("s b u e -> s b e u"))
 
-        def clock(which):
-            tick = sb([P, 1], F32, "tick_" + which)
-            source = {"max": lambda: made["neg_max"][:], "w": lambda: w_grouped[:, 0, 0:1], "kg": lambda: km_grouped[1][:, 0, 0:1],
-                      "inv": lambda: made["inv_sum"][:], "p": lambda: made["p"][:, 0, 0, 0:1]}[which]()
-            nc.gpsimd.tensor_copy(tick[:], source)
+        w_codes = sbuf([P, Q], U32, "w_codes")
+        w_scales = sbuf([P, Q], U8, "w_scales")
+        low_codes = sbuf([P, 2 * P], U32, "low_codes")
+        low_scales = sbuf([P, 2 * P], U8, "low_scales")
+        high_codes = sbuf([P, 2 * P], U32, "high_codes")
+        high_scales = sbuf([P, 2 * P], U8, "high_scales")
+        block2, block3 = slice(0, P), slice(P, 2 * P)
+        quantise(high_codes[:, block3], high_scales[:, block3], v_high[:, 1, :, :].rearrange("s e t -> s (e t)"))
+        quantise(low_codes[:], low_scales[:], v_low[:].rearrange("s b e t -> s (b e t)"))
+        quantise(w_codes[:], w_scales[:], w_grouped[:].rearrange("s b q t -> s (b q t)"))
+        quantise(high_codes[:, block2], high_scales[:, block2], v_high[:, 0, :, :].rearrange("s e t -> s (e t)"))
 
-        sig(0)
-        mul(0)
-        sig(1)
-        sig(2)
-        mul(1)
-        weavepair(0, 0)
-        weavepair(1, 0)
-        sig(3)
-        warmexp()
-        mul(2)
-        qcopy("S")
-        qquant()
-        mul(3)
-        weavepair(0, 1)
-        weavepair(1, 1)
-        kquant(0)
-        kquant(1)
-        score(0)
-        score(1)
-        cast(0)
-        picks(0)
-        vturn(0, 0)
-        pickv(1, "km_grouped0")
-        vturn(1, 0)
-        rowmax("val_bf0")
-        cast(2)
-        pickv(3)
-        vturn(3, 1)
-        expo()
-        picks(2)
-        vturn(2, 2)
-        recip()
-        weigh(0)
-        weigh(1)
-        vcopy(3, 1, "S")
-        wcopy()
-        vcopypair(0, 0, "V", "row_sum")
-        vcopy(2, 2, "V")
-        vquantpair(0)
-        vquantpair(1)
-        wquant()
-        outp(0, "S")
-        outp(1, "V")
+        acc_low = bank([Q, 2 * P], "acc_low")
+        product(acc_low[:], w_codes[:], w_scales[:], low_codes[:], low_scales[:])
+        out_low = sbuf([Q, 2 * P], F32, "out_low")
+        nc.vector.tensor_copy(out_low[:], acc_low[:])
+        nc.sync.dma_start(out[:, 0 : 2 * P], out_low[:])
+
+        out_high = sbuf([Q, 2 * P], F32, "out_high")
+        for cols, acc in ((block3, bank([Q, P], "acc3")), (block2, bank([Q, P], "acc2", "scores"))):
+            product(acc[:], w_codes[:], w_scales[:], high_codes[:, cols], high_scales[:, cols])
+            nc.scalar.copy(out_high[:, cols], acc[:])
+        nc.scalar.dma_start(out[:, 2 * P : 4 * P], out_high[:])

from contextlib import ExitStack

import concourse.mybir as mybir
from concourse.masks import make_identity

D, T, I, Q, E = 512, 1024, 512, 128, 512
FLOPS = 2 * Q * I * D + 2 * Q * I * E

F32 = mybir.dt.float32
BF16 = mybir.dt.bfloat16
U32 = mybir.dt.uint32
U16 = mybir.dt.uint16
U8 = mybir.dt.uint8
FP8X4 = mybir.dt.float8_e4m3fn_x4
ACT = mybir.ActivationFunctionType
ALU = mybir.AluOpType

P = 128
PACK = 4
HALF = I // 2
LIST_ROWS = 16
ALIGN = 256


def tile_attend_gatedkeys_kernel(tc, query, keys, kgate, size, vals, offs, out):
    nc = tc.nc
    with ExitStack() as ctx:
        keep = ctx.enter_context(tc.tile_pool(name="keep", bufs=1))
        psum = ctx.enter_context(tc.psum_pool(name="psum", bufs=1))

        def sbuf(shape, dtype, name, in_place_of=None):
            return keep.tile(shape, dtype, name=name, tag=in_place_of or name, align_bytes=ALIGN)

        def bank(shape, name, in_place_of=None):
            return psum.tile(shape, F32, name=name, tag=in_place_of or name)

        def quantise(codes, scales, grouped):
            nc.vector.quantize_mx(codes.bitcast(FP8X4), scales, grouped)

        def product(acc, lhs_codes, lhs_scales, rhs_codes, rhs_scales):
            nc.tensor.matmul_mx(acc, lhsT=lhs_codes.bitcast(FP8X4), lhsT_scale=lhs_scales,
                                rhs=rhs_codes.bitcast(FP8X4), rhs_scale=rhs_scales, start=True, stop=True)

        offsets = keep.tile([P, I // LIST_ROWS], U16, name="offsets")
        gate_pool = [sbuf([P, T], F32, "gate_pool%d" % t) for t in range(PACK)]
        key_pool = [sbuf([P, T], F32, "key_pool%d" % t) for t in range(PACK)]
        val_pool = [sbuf([P, T], F32, "val_pool%d" % b) for b in range(E // P)]
        query_raw = sbuf([P, PACK, Q], F32, "query_raw")
        size_cols = sbuf([P, PACK], F32, "size_cols")
        gate_planes = kgate.rearrange("(p t) n -> t p n", t=PACK)
        key_planes = keys.rearrange("(p t) n -> t p n", t=PACK)

        nc.sync.dma_start(gate_pool[0][:], gate_planes[0])
        nc.sync.dma_start(offsets[:], offs)
        nc.sync.dma_start(key_pool[0][:], key_planes[0])
        nc.sync.dma_start(gate_pool[1][:], gate_planes[1])
        for t in range(1, PACK - 1):
            nc.sync.dma_start(gate_pool[t + 1][:], gate_planes[t + 1])
            nc.sync.dma_start(key_pool[t][:], key_planes[t])
        nc.sync.dma_start(key_pool[PACK - 1][:], key_planes[PACK - 1])
        nc.sync.dma_start(query_raw[:], query.rearrange("(p t) q -> p t q", t=PACK))
        nc.sync.dma_start(size_cols[:], size.rearrange("o (s t) -> s (o t)", t=PACK))
        for b in range(E // P):
            nc.sync.dma_start(val_pool[b][:], vals[b * P : (b + 1) * P, :])

        ident = sbuf([P, P], F32, "ident")
        make_identity(nc, ident[:])
        size_rows = bank([P, PACK, P], "size_rows")
        for t in range(PACK):
            nc.tensor.transpose(size_rows[:, t, :], size_cols[:, t : t + 1].to_broadcast([P, P]), ident[:])

        km = [sbuf([P, PACK, HALF], F32, "km%d" % h) for h in range(2)]
        km_grouped = [sbuf([P, HALF, PACK], BF16, "km_grouped%d" % h) for h in range(2)]
        km_codes = [sbuf([P, HALF], U32, "km_codes%d" % h) for h in range(2)]
        km_scales = [sbuf([P, HALF], U8, "km_scales%d" % h) for h in range(2)]
        gates = [sbuf([P, I], F32, "gate%d" % t) for t in range(PACK)]

        def gather_gates(t):
            nc.scalar.activation(gates[t][:], gate_pool[t][:].indirect(offsets[:]), ACT.Sigmoid)

        def gather_keys(t):
            for h in range(2):
                entries = offsets[:, h * HALF // LIST_ROWS : (h + 1) * HALF // LIST_ROWS]
                nc.vector.tensor_tensor(km[h][:, t, :], key_pool[t][:].indirect(entries),
                                        gates[t][:, h * HALF : (h + 1) * HALF], ALU.mult)

        def group_planes(first):
            for h in range(2):
                nc.vector.tensor_copy(km_grouped[h][:, :, first : first + 2],
                                      km[h][:, first : first + 2, :].rearrange("p t i -> p i t"))

        gather_gates(0)
        gather_keys(0)
        gather_gates(1)
        gather_gates(2)
        gather_keys(1)
        group_planes(0)
        gather_gates(3)
        warm_exp = sbuf([P, 1], F32, "warm_exp")
        nc.scalar.activation(warm_exp[:], gates[PACK - 1][:, 0:1], ACT.Exp)
        gather_keys(2)
        gather_keys(3)

        q_grouped = sbuf([P, Q, PACK], BF16, "q_grouped")
        q_codes = sbuf([P, Q], U32, "q_codes")
        q_scales = sbuf([P, Q], U8, "q_scales")
        nc.scalar.copy(q_grouped[:].rearrange("p (c j) t -> p c t j", j=4),
                       query_raw[:].rearrange("p t (c j) -> p c t j", j=4))
        group_planes(2)
        quantise(km_codes[0][:], km_scales[0][:], km_grouped[0][:].rearrange("p i t -> p (i t)"))
        quantise(q_codes[:], q_scales[:], q_grouped[:].rearrange("p q t -> p (q t)"))
        quantise(km_codes[1][:], km_scales[1][:], km_grouped[1][:].rearrange("p i t -> p (i t)"))

        scores = bank([Q, I], "scores")
        for h in range(2):
            product(scores[:, h * HALF : (h + 1) * HALF], q_codes[:], q_scales[:], km_codes[h][:], km_scales[h][:])

        def cast_values(b):
            val_bf = sbuf([P, T], BF16, "val_bf%d" % b)
            nc.scalar.activation(val_bf[:], val_pool[b][:], ACT.Copy)
            return val_bf

        def gather_values_scalar(b, val_bf):
            picked = sbuf([P, I], BF16, "picked%d" % b)
            nc.scalar.activation(picked[:], val_bf[:].indirect(offsets[:]), ACT.Copy)
            return picked

        def gather_values_vector(b, in_place_of=None):
            picked = sbuf([P, I], BF16, "picked%d" % b, in_place_of)
            nc.vector.tensor_copy(picked[:], val_pool[b][:].indirect(offsets[:]))
            return picked

        def turn_values(turned, picked):
            pairs = picked[:].bitcast(F32)
            for u in range(2):
                nc.tensor.transpose(turned[:, u, :], pairs[:, u : I // 2 : 2], ident[:])

        turned_low = bank([P, 2, 2, P], "turned_low")
        turn_values(turned_low[:, 0, :, :], gather_values_scalar(0, cast_values(0)))
        turn_values(turned_low[:, 1, :, :], gather_values_vector(1, "km_grouped0"))

        neg_max = sbuf([Q, 1], F32, "neg_max", "val_bf0")
        nc.vector.tensor_reduce(neg_max[:], scores[:], mybir.AxisListType.X, ALU.max, negate=True)

        val_bf2 = cast_values(2)
        turned3 = bank([P, 2, P], "turned3")
        turn_values(turned3[:], gather_values_vector(3))

        p_dealt = sbuf([Q, 2, P, 2], F32, "p_dealt")
        row_sum = sbuf([Q, 1], F32, "row_sum")
        nc.scalar.activation(p_dealt[:], scores[:].rearrange("q (s u j) -> q u s j", u=2, j=2), ACT.Exp,
                             bias=neg_max[:], accum_out=row_sum[:])
        picked2 = gather_values_scalar(2, val_bf2)

        inv_sum = sbuf([Q, 1], F32, "inv_sum")
        nc.vector.reciprocal(inv_sum[:], row_sum[:])
        w_turned = bank([P, 2, Q], "w_turned")
        for u in range(2):
            w_pairs = sbuf([Q, P, 2], BF16, "w_pairs%d" % u)
            nc.vector.scalar_tensor_tensor(w_pairs[:], p_dealt[:, u, :, :], inv_sum[:],
                                           size_rows[:, 2 * u : 2 * u + 2, :].rearrange("q j s -> q s j"),
                                           ALU.mult, ALU.mult)
            nc.tensor.transpose(w_turned[:, u, :], w_pairs[:].rearrange("q s j -> q (s j)").bitcast(F32), ident[:])

        turned2 = bank([P, 2, P], "turned2", "size_rows")
        turn_values(turned2[:], picked2)

        def as_pairs(grouped):
            blocks = grouped.shape[1]
            words = grouped[:].rearrange("s b c t -> s (b c t)").bitcast(F32)
            return words.rearrange("s (b c u) -> s b c u", b=blocks, u=2)

        v_high = sbuf([P, 2, P, PACK], BF16, "v_high")
        w_grouped = sbuf([P, 1, Q, PACK], BF16, "w_grouped")
        nc.scalar.copy(as_pairs(v_high)[:, 1, :, :], turned3[:].rearrange("s u e -> s e u"))
        nc.scalar.copy(as_pairs(w_grouped)[:, 0, :, :], w_turned[:].rearrange("s u q -> s q u"))
        nc.scalar.copy(as_pairs(v_high)[:, 0, :, :], turned2[:].rearrange("s u e -> s e u"))
        v_low = sbuf([P, 2, P, PACK], BF16, "v_low", "row_sum")
        nc.vector.tensor_copy(as_pairs(v_low), turned_low[:].rearrange("s b u e -> s b e u"))

        w_codes = sbuf([P, Q], U32, "w_codes")
        w_scales = sbuf([P, Q], U8, "w_scales")
        low_codes = sbuf([P, 2 * P], U32, "low_codes")
        low_scales = sbuf([P, 2 * P], U8, "low_scales")
        high_codes = sbuf([P, 2 * P], U32, "high_codes")
        high_scales = sbuf([P, 2 * P], U8, "high_scales")
        block2, block3 = slice(0, P), slice(P, 2 * P)
        quantise(high_codes[:, block3], high_scales[:, block3], v_high[:, 1, :, :].rearrange("s e t -> s (e t)"))
        quantise(low_codes[:], low_scales[:], v_low[:].rearrange("s b e t -> s (b e t)"))
        quantise(w_codes[:], w_scales[:], w_grouped[:].rearrange("s b q t -> s (b q t)"))
        quantise(high_codes[:, block2], high_scales[:, block2], v_high[:, 0, :, :].rearrange("s e t -> s (e t)"))

        acc_low = bank([Q, 2 * P], "acc_low")
        product(acc_low[:], w_codes[:], w_scales[:], low_codes[:], low_scales[:])
        out_low = sbuf([Q, 2 * P], F32, "out_low")
        nc.vector.tensor_copy(out_low[:], acc_low[:])
        nc.sync.dma_start(out[:, 0 : 2 * P], out_low[:])

        out_high = sbuf([Q, 2 * P], F32, "out_high")
        for cols, acc in ((block3, bank([Q, P], "acc3")), (block2, bank([Q, P], "acc2", "scores"))):
            product(acc[:], w_codes[:], w_scales[:], high_codes[:, cols], high_scales[:, cols])
            nc.scalar.copy(out_high[:, cols], acc[:])
        nc.scalar.dma_start(out[:, 2 * P : 4 * P], out_high[:])
